import numpy as np
import ml_dtypes


def mxq(x, axis, fmt="e4m3"):
    dtype, down = {"e4m3": (ml_dtypes.float8_e4m3fn, 7), "e5m2": (ml_dtypes.float8_e5m2, 14)}[fmt]
    v = np.moveaxis(np.asarray(x, np.float32).astype(ml_dtypes.bfloat16).astype(np.float64), axis, -1)
    blocks = v.reshape(v.shape[:-1] + (-1, 32))
    amax = np.abs(blocks).max(-1, keepdims=True)
    byte = np.maximum(np.where(amax > 0, np.frexp(amax)[1] - 1 + 127, 0) - down, 1)
    scale = np.exp2(byte - 127.0)
    codes = (blocks / scale).astype(np.float32).astype(dtype).astype(np.float64)
    return np.moveaxis((codes * scale).reshape(v.shape), -1, axis)


WIDE = False


def mx_kscale(k):
    if not WIDE:
        return np.ones(k)
    levels = np.array([10, -10, 5, -5, 0])
    if k % 512:
        return np.exp2(np.random.permutation(np.resize(levels, k // 32))).repeat(32)
    a = np.empty((k // 512, 16))
    for p in range(k // 512):
        a[p, :8] = np.random.permutation(np.resize(levels, 8))
        for g in range(8):
            far = levels[np.abs(levels - a[p, g]) >= 10]
            a[p, g + 8] = far[np.random.randint(len(far))]
    return np.exp2(a.ravel()).repeat(32)


def f64(x):
    return np.asarray(x).astype(np.float64)


def striped(idx):
    return np.tile(idx.reshape(-1, 16).T, (8, 1)).astype(np.uint16)


def unstriped(offs):
    return offs[:16].T.reshape(-1).astype(np.int64)


def pack_weight(w):
    k, n = w.shape
    w = f64(np.asarray(w, np.float32).astype(ml_dtypes.bfloat16)).reshape(k // 32, 32, n)
    amax = np.abs(w).max(1)
    byte = np.clip(np.where(amax > 0, np.frexp(amax)[1] - 1 + 127 - 7, 1), 1, 254)
    scaled = (w * np.exp2(127.0 - byte)[:, None, :]).reshape(k, n).astype(np.float32)
    words = np.ascontiguousarray(scaled.reshape(k // 512, 128, 4, n).transpose(0, 1, 3, 2)).astype(ml_dtypes.float8_e4m3fn).view(np.uint8)
    return words, np.ascontiguousarray(byte.astype(np.uint8).reshape(k // 512, 16, n))


def unpack_weight(words, scales):
    g, p, n, _ = words.shape
    vals = np.ascontiguousarray(words).view(ml_dtypes.float8_e4m3fn).astype(np.float64) * np.repeat(np.exp2(scales.astype(np.float64) - 127.0), 8, axis=1)[..., None]
    return vals.transpose(0, 1, 3, 2).reshape(g * 512, n)


def sigmoid(v):
    return 1.0 / (1.0 + np.exp(-np.maximum(v, -700.0)))


K, T, S, N = 512, 1024, 512, 256


def setup_inputs():
    n = np.random.standard_normal
    s = mx_kscale(K)[:, None]
    packed_w1 = pack_weight(n((K, N)) / np.sqrt(K) / s)
    return {
        "xT": (n((K, T)) * s).astype(np.float32),
        "side": n((N, T)).astype(np.float32),
        "w1_words": packed_w1[0],
        "w1_scales": packed_w1[1],
        "offs": striped(np.random.permutation(T)[:S]),
    }


def reference(xT, side, w1_words, w1_scales, offs):
    xq = mxq(f64(xT)[:, unstriped(offs)], 0, "e4m3")
    y = unpack_weight(w1_words, w1_scales).T @ xq
    g = f64(side)[:, unstriped(offs)]
    return y * sigmoid(g)

@@ -1,0 +1,105 @@
+from contextlib import ExitStack
+
+import concourse.mybir as mybir
+
+K, T, S, N = 512, 1024, 512, 256
+FLOPS = 2 * K * S * N
+
+F32 = mybir.dt.float32
+BF16 = mybir.dt.bfloat16
+I32 = mybir.dt.int32
+U32 = mybir.dt.uint32
+U16 = mybir.dt.uint16
+U8 = mybir.dt.uint8
+FP8X4 = mybir.dt.float8_e4m3fn_x4
+SIGMOID = mybir.ActivationFunctionType.Sigmoid
+MULT = mybir.AluOpType.mult
+
+P = 128
+PACK = 4
+HALF = S // 2
+LANES = 16
+
+
+def tile_picked_sidegate_sigmoid_l_kernel(tc, xT, side, w1_words, w1_scales, offs, out):
+    nc = tc.nc
+    with ExitStack() as ctx:
+        keep = ctx.enter_context(tc.tile_pool(name="keep", bufs=1))
+        psum = ctx.enter_context(tc.psum_pool(name="psum", bufs=1))
+
+        offsets = keep.tile([P, S // LANES], U16, name="offsets")
+        planes = [keep.tile([P, T], F32, name=f"plane{t}") for t in range(PACK)]
+        sides = [keep.tile([P, T], F32, name=f"side{b}") for b in range(N // P)]
+        w_codes = keep.tile([P, N], U32, name="w_codes", align_bytes=64)
+        w_scales = keep.tile([P, N], U8, name="w_scales", align_bytes=64)
+        x_rows = xT.rearrange("(p t) c -> p t c", t=PACK)
+
+        for q in range(4):
+            nc.scalar.dma_start(
+                out=w_scales[32 * q : 32 * q + 4, :].bitcast(I32),
+                in_=w1_scales[0, 4 * q : 4 * q + 4, :].bitcast(I32),
+            )
+        nc.sync.dma_start(out=planes[0][:], in_=x_rows[:, 0, :])
+        nc.sync.dma_start(offsets[:], offs)
+        for t in range(1, PACK):
+            nc.sync.dma_start(out=planes[t][:], in_=x_rows[:, t, :])
+        nc.sync.dma_start(
+            out=w_codes[:].bitcast(I32),
+            in_=w1_words[0].rearrange("p n t -> p (n t)").bitcast(I32),
+        )
+        for b in range(N // P):
+            nc.sync.dma_start(out=sides[b][:], in_=side[b * P : (b + 1) * P, :])
+
+        gates = [keep.tile([P, S], F32, name=f"gate{b}") for b in range(N // P)]
+        zero = keep.tile([P, 1], F32, name="zero")
+        nc.vector.memset(zero[:], 0.0)
+        nc.scalar.activation(gates[0][:, 0:1], zero[:], SIGMOID)
+
+        def cols(h):
+            return slice(h * HALF, (h + 1) * HALF)
+
+        def entries(h):
+            return offsets[:, h * HALF // LANES : (h + 1) * HALF // LANES]
+
+        low = keep.tile([P, 2, S], F32, name="low")
+        high = keep.tile([P, 2, S], F32, name="high")
+        woven = [keep.tile([P, HALF, PACK], BF16, name=f"woven{h}", align_bytes=64) for h in range(2)]
+        x_codes = [keep.tile([P, HALF], U32, name=f"x_codes{h}", align_bytes=64) for h in range(2)]
+        x_scales = [keep.tile([P, HALF], U8, name=f"x_scales{h}", align_bytes=64) for h in range(2)]
+
+        nc.vector.tensor_copy(low[:, 0, :], planes[0][:].indirect(offsets[:]))
+        nc.vector.tensor_copy(low[:, 1, :], planes[1][:].indirect(offsets[:]))
+        for h in range(2):
+            nc.scalar.copy(woven[h][:, :, 0:2], low[:, :, cols(h)].rearrange("p t s -> p s t"))
+        nc.vector.tensor_copy(high[:, 0, :], planes[2][:].indirect(offsets[:]))
+        for h in range(2):
+            nc.vector.tensor_copy(high[:, 1, cols(h)], planes[3][:].indirect(entries(h)))
+        for h in range(2):
+            nc.vector.tensor_copy(woven[h][:, :, 2:4], high[:, :, cols(h)].rearrange("p t s -> p s t"))
+        for h in range(2):
+            nc.vector.quantize_mx(
+                out=x_codes[h][:].bitcast(FP8X4),
+                scales=x_scales[h][:],
+                in_=woven[h][:].rearrange("p s t -> p (s t)"),
+            )
+
+        nc.scalar.activation(gates[0][:], sides[0][:].indirect(offsets[:]), SIGMOID)
+        for h in range(2):
+            nc.scalar.activation(gates[1][:, cols(h)], sides[1][:].indirect(entries(h)), SIGMOID)
+
+        results = [keep.tile([P, S], F32, name=f"result{b}") for b in range(N // P)]
+        for b in range(N // P):
+            rows = slice(b * P, (b + 1) * P)
+            for h in range(2):
+                acc = psum.tile([P, HALF], F32, name=f"acc{b}{h}")
+                nc.tensor.matmul_mx(
+                    out=acc[:],
+                    lhsT=w_codes[:, rows].bitcast(FP8X4),
+                    lhsT_scale=w_scales[:, rows],
+                    rhs=x_codes[h][:].bitcast(FP8X4),
+                    rhs_scale=x_scales[h][:],
+                    start=True,
+                    stop=True,
+                )
+                nc.vector.tensor_tensor(results[b][:, cols(h)], acc[:], gates[b][:, cols(h)], MULT)
+                nc.sync.dma_start(out=out[rows, cols(h)], in_=results[b][:, cols(h)])

@@ -13,6 +13,7 @@ U16 = mybir.dt.uint16
 U8 = mybir.dt.uint8
 FP8X4 = mybir.dt.float8_e4m3fn_x4
 SIGMOID = mybir.ActivationFunctionType.Sigmoid
+COPY = mybir.ActivationFunctionType.Copy
 MULT = mybir.AluOpType.mult
 
 P = 128
@@ -39,16 +40,16 @@ def tile_picked_sidegate_sigmoid_l_kernel(tc, xT, side, w1_words, w1_scales, off
                 out=w_scales[32 * q : 32 * q + 4, :].bitcast(I32),
                 in_=w1_scales[0, 4 * q : 4 * q + 4, :].bitcast(I32),
             )
-        nc.sync.dma_start(out=planes[0][:], in_=x_rows[:, 0, :])
+        nc.sync.dma_start(out=planes[2][:], in_=x_rows[:, 2, :])
         nc.sync.dma_start(offsets[:], offs)
-        for t in range(1, PACK):
+        for t in (0, 1, 3):
             nc.sync.dma_start(out=planes[t][:], in_=x_rows[:, t, :])
+        nc.sync.dma_start(out=sides[0][:], in_=side[0:P, :])
         nc.sync.dma_start(
             out=w_codes[:].bitcast(I32),
             in_=w1_words[0].rearrange("p n t -> p (n t)").bitcast(I32),
         )
-        for b in range(N // P):
-            nc.sync.dma_start(out=sides[b][:], in_=side[b * P : (b + 1) * P, :])
+        nc.sync.dma_start(out=sides[1][:], in_=side[P : 2 * P, :])
 
         gates = [keep.tile([P, S], F32, name=f"gate{b}") for b in range(N // P)]
         zero = keep.tile([P, 1], F32, name="zero")
@@ -61,21 +62,22 @@ def tile_picked_sidegate_sigmoid_l_kernel(tc, xT, side, w1_words, w1_scales, off
         def entries(h):
             return offsets[:, h * HALF // LANES : (h + 1) * HALF // LANES]
 
-        low = keep.tile([P, 2, S], F32, name="low")
-        high = keep.tile([P, 2, S], F32, name="high")
+        low = [keep.tile([P, 2, HALF], BF16, name=f"low{h}") for h in range(2)]
+        rounded = keep.tile([P, T], BF16, name="rounded")
         woven = [keep.tile([P, HALF, PACK], BF16, name=f"woven{h}", align_bytes=64) for h in range(2)]
         x_codes = [keep.tile([P, HALF], U32, name=f"x_codes{h}", align_bytes=64) for h in range(2)]
         x_scales = [keep.tile([P, HALF], U8, name=f"x_scales{h}", align_bytes=64) for h in range(2)]
 
-        nc.vector.tensor_copy(low[:, 0, :], planes[0][:].indirect(offsets[:]))
-        nc.vector.tensor_copy(low[:, 1, :], planes[1][:].indirect(offsets[:]))
         for h in range(2):
-            nc.scalar.copy(woven[h][:, :, 0:2], low[:, :, cols(h)].rearrange("p t s -> p s t"))
-        nc.vector.tensor_copy(high[:, 0, :], planes[2][:].indirect(offsets[:]))
+            nc.vector.tensor_copy(woven[h][:, :, 2], planes[2][:].indirect(entries(h)))
+        nc.vector.tensor_copy(low[0][:, 0, :], planes[0][:].indirect(entries(0)))
+        nc.scalar.copy(rounded[:], planes[0][:])
+        nc.scalar.activation(low[1][:, 0, :], rounded[:].indirect(entries(1)), COPY)
         for h in range(2):
-            nc.vector.tensor_copy(high[:, 1, cols(h)], planes[3][:].indirect(entries(h)))
+            nc.vector.tensor_copy(low[h][:, 1, :], planes[1][:].indirect(entries(h)))
+            nc.scalar.copy(woven[h][:, :, 0:2], low[h][:].rearrange("p t s -> p s t"))
         for h in range(2):
-            nc.vector.tensor_copy(woven[h][:, :, 2:4], high[:, :, cols(h)].rearrange("p t s -> p s t"))
+            nc.vector.tensor_copy(woven[h][:, :, 3], planes[3][:].indirect(entries(h)))
         for h in range(2):
             nc.vector.quantize_mx(
                 out=x_codes[h][:].bitcast(FP8X4),

@@ -20,6 +20,8 @@ P = 128
 PACK = 4
 HALF = S // 2
 LANES = 16
+DIRECT = 224
+LAST_CUTS = (0, 256, 416, 512)
 
 
 def tile_picked_sidegate_sigmoid_l_kernel(tc, xT, side, w1_words, w1_scales, offs, out):
@@ -34,74 +36,91 @@ def tile_picked_sidegate_sigmoid_l_kernel(tc, xT, side, w1_words, w1_scales, off
         w_codes = keep.tile([P, N], U32, name="w_codes", align_bytes=64)
         w_scales = keep.tile([P, N], U8, name="w_scales", align_bytes=64)
         x_rows = xT.rearrange("(p t) c -> p t c", t=PACK)
+        gates = [keep.tile([P, S], F32, name=f"gate{b}") for b in range(N // P)]
+        zero = keep.tile([P, 1], F32, name="zero")
 
-        for q in range(4):
-            nc.scalar.dma_start(
+        def load_scales(q, queue):
+            queue.dma_start(
                 out=w_scales[32 * q : 32 * q + 4, :].bitcast(I32),
                 in_=w1_scales[0, 4 * q : 4 * q + 4, :].bitcast(I32),
             )
-        nc.sync.dma_start(out=planes[2][:], in_=x_rows[:, 2, :])
-        nc.sync.dma_start(offsets[:], offs)
-        for t in (0, 1, 3):
-            nc.sync.dma_start(out=planes[t][:], in_=x_rows[:, t, :])
-        nc.sync.dma_start(out=sides[0][:], in_=side[0:P, :])
-        nc.sync.dma_start(
-            out=w_codes[:].bitcast(I32),
-            in_=w1_words[0].rearrange("p n t -> p (n t)").bitcast(I32),
-        )
-        nc.sync.dma_start(out=sides[1][:], in_=side[P : 2 * P, :])
 
-        gates = [keep.tile([P, S], F32, name=f"gate{b}") for b in range(N // P)]
-        zero = keep.tile([P, 1], F32, name="zero")
-        nc.vector.memset(zero[:], 0.0)
-        nc.scalar.activation(gates[0][:, 0:1], zero[:], SIGMOID)
-
-        def cols(h):
-            return slice(h * HALF, (h + 1) * HALF)
-
-        def entries(h):
-            return offsets[:, h * HALF // LANES : (h + 1) * HALF // LANES]
-
-        low = [keep.tile([P, 2, HALF], BF16, name=f"low{h}") for h in range(2)]
-        rounded = keep.tile([P, T], BF16, name="rounded")
-        woven = [keep.tile([P, HALF, PACK], BF16, name=f"woven{h}", align_bytes=64) for h in range(2)]
-        x_codes = [keep.tile([P, HALF], U32, name=f"x_codes{h}", align_bytes=64) for h in range(2)]
-        x_scales = [keep.tile([P, HALF], U8, name=f"x_scales{h}", align_bytes=64) for h in range(2)]
-
-        for h in range(2):
-            nc.vector.tensor_copy(woven[h][:, :, 2], planes[2][:].indirect(entries(h)))
-        nc.vector.tensor_copy(low[0][:, 0, :], planes[0][:].indirect(entries(0)))
-        nc.scalar.copy(rounded[:], planes[0][:])
-        nc.scalar.activation(low[1][:, 0, :], rounded[:].indirect(entries(1)), COPY)
-        for h in range(2):
-            nc.vector.tensor_copy(low[h][:, 1, :], planes[1][:].indirect(entries(h)))
-            nc.scalar.copy(woven[h][:, :, 0:2], low[h][:].rearrange("p t s -> p s t"))
-        for h in range(2):
-            nc.vector.tensor_copy(woven[h][:, :, 3], planes[3][:].indirect(entries(h)))
-        for h in range(2):
-            nc.vector.quantize_mx(
-                out=x_codes[h][:].bitcast(FP8X4),
-                scales=x_scales[h][:],
-                in_=woven[h][:].rearrange("p s t -> p (s t)"),
+        def load_words(queue):
+            queue.dma_start(
+                out=w_codes[:].bitcast(I32),
+                in_=w1_words[0].rearrange("p n t -> p (n t)").bitcast(I32),
             )
 
-        nc.scalar.activation(gates[0][:], sides[0][:].indirect(offsets[:]), SIGMOID)
-        for h in range(2):
-            nc.scalar.activation(gates[1][:, cols(h)], sides[1][:].indirect(entries(h)), SIGMOID)
+        def warm_up():
+            nc.vector.memset(zero[:], 0.0)
+            nc.scalar.activation(gates[0][:, 0:1], zero[:], SIGMOID)
+
+        for q in range(4):
+            load_scales(q, nc.scalar)
+        nc.sync.dma_start(out=planes[0][:], in_=x_rows[:, 0, :])
+        nc.sync.dma_start(offsets[:], offs)
+        for t in (1, 2, 3):
+            nc.sync.dma_start(out=planes[t][:], in_=x_rows[:, t, :])
+        nc.sync.dma_start(out=sides[0][:], in_=side[0:P, :])
+        load_words(nc.sync)
+        nc.sync.dma_start(out=sides[1][:], in_=side[P : 2 * P, :])
+        warm_up()
+
+        def entries(lo, hi):
+            return offsets[:, lo // LANES : hi // LANES]
+
+        x_codes = keep.tile([P, S], U32, name="x_codes", align_bytes=64)
+        x_scales = keep.tile([P, S], U8, name="x_scales", align_bytes=64)
+        low = [keep.tile([P, 2, S - DIRECT], BF16, name=f"low{u}") for u in range(2)]
+        woven = keep.tile([P, S, PACK], BF16, name="woven", align_bytes=64)
+
+        for t in range(PACK):
+            u = t // 2
+            nc.vector.tensor_copy(woven[:, 0:DIRECT, t], planes[t][:].indirect(entries(0, DIRECT)))
+            nc.scalar.activation(low[u][:, t % 2, :], planes[t][:].indirect(entries(DIRECT, S)), COPY)
+            if t % 2 == 1:
+                cuts = (DIRECT, HALF, S) if u == 1 else (DIRECT, S)
+                for lo, hi in zip(cuts, cuts[1:]):
+                    nc.vector.tensor_copy(
+                        woven[:, lo:hi, 2 * u : 2 * u + 2],
+                        low[u][:, :, lo - DIRECT : hi - DIRECT].rearrange("p t s -> p s t"),
+                    )
+        for lo in (0, HALF):
+            nc.vector.quantize_mx(
+                out=x_codes[:, lo : lo + HALF].bitcast(FP8X4),
+                scales=x_scales[:, lo : lo + HALF],
+                in_=woven[:, lo : lo + HALF, :].rearrange("p s t -> p (s t)"),
+            )
 
         results = [keep.tile([P, S], F32, name=f"result{b}") for b in range(N // P)]
+
+        def gate(b, lo, hi):
+            nc.scalar.activation(gates[b][:, lo:hi], sides[b][:].indirect(entries(lo, hi)), SIGMOID)
+
+        def product(b, lo, hi):
+            acc = psum.tile([P, hi - lo], F32, name=f"acc{b}_{lo}")
+            nc.tensor.matmul_mx(
+                out=acc[:],
+                lhsT=w_codes[:, b * P : (b + 1) * P].bitcast(FP8X4),
+                lhsT_scale=w_scales[:, b * P : (b + 1) * P],
+                rhs=x_codes[:, lo:hi].bitcast(FP8X4),
+                rhs_scale=x_scales[:, lo:hi],
+                start=True,
+                stop=True,
+            )
+            return acc
+
+        def store(b, lo, hi):
+            nc.sync.dma_start(out=out[b * P : (b + 1) * P, lo:hi], in_=results[b][:, lo:hi])
+
+        for lo in (0, HALF):
+            gate(0, lo, lo + HALF)
+        for lo, hi in zip(LAST_CUTS, LAST_CUTS[1:]):
+            gate(1, lo, hi)
         for b in range(N // P):
-            rows = slice(b * P, (b + 1) * P)
-            for h in range(2):
-                acc = psum.tile([P, HALF], F32, name=f"acc{b}{h}")
-                nc.tensor.matmul_mx(
-                    out=acc[:],
-                    lhsT=w_codes[:, rows].bitcast(FP8X4),
-                    lhsT_scale=w_scales[:, rows],
-                    rhs=x_codes[h][:].bitcast(FP8X4),
-                    rhs_scale=x_scales[h][:],
-                    start=True,
-                    stop=True,
-                )
-                nc.vector.tensor_tensor(results[b][:, cols(h)], acc[:], gates[b][:, cols(h)], MULT)
-                nc.sync.dma_start(out=out[rows, cols(h)], in_=results[b][:, cols(h)])
+            for lo in (0, HALF):
+                acc = product(b, lo, lo + HALF)
+                cuts = LAST_CUTS[1:] if b == 1 and lo == HALF else (lo, lo + HALF)
+                for c0, c1 in zip(cuts, cuts[1:]):
+                    nc.vector.tensor_tensor(results[b][:, c0:c1], acc[:, c0 - lo : c1 - lo], gates[b][:, c0:c1], MULT)
+                store(b, lo, lo + HALF)

@@ -21,6 +21,7 @@ PACK = 4
 HALF = S // 2
 LANES = 16
 DIRECT = 224
+MIDDLE = 384
 LAST_CUTS = (0, 256, 416, 512)
 
 
@@ -77,13 +78,13 @@ def tile_picked_sidegate_sigmoid_l_kernel(tc, xT, side, w1_words, w1_scales, off
         for t in range(PACK):
             u = t // 2
             nc.vector.tensor_copy(woven[:, 0:DIRECT, t], planes[t][:].indirect(entries(0, DIRECT)))
-            nc.scalar.activation(low[u][:, t % 2, :], planes[t][:].indirect(entries(DIRECT, S)), COPY)
-            if t % 2 == 1:
-                cuts = (DIRECT, HALF, S) if u == 1 else (DIRECT, S)
-                for lo, hi in zip(cuts, cuts[1:]):
+            cuts = (DIRECT, MIDDLE, S) if t == PACK - 1 else (DIRECT, S)
+            for lo, hi in zip(cuts, cuts[1:]):
+                part = slice(lo - DIRECT, hi - DIRECT)
+                nc.scalar.activation(low[u][:, t % 2, part], planes[t][:].indirect(entries(lo, hi)), COPY)
+                if t % 2 == 1:
                     nc.vector.tensor_copy(
-                        woven[:, lo:hi, 2 * u : 2 * u + 2],
-                        low[u][:, :, lo - DIRECT : hi - DIRECT].rearrange("p t s -> p s t"),
+                        woven[:, lo:hi, 2 * u : 2 * u + 2], low[u][:, :, part].rearrange("p t s -> p s t")
                     )
         for lo in (0, HALF):
             nc.vector.quantize_mx(

@@ -18,11 +18,12 @@ MULT = mybir.AluOpType.mult
 
 P = 128
 PACK = 4
-HALF = S // 2
+QUADRANT = 32
 LANES = 16
+HALF = S // 2
 DIRECT = 224
 MIDDLE = 384
-LAST_CUTS = (0, 256, 416, 512)
+TAIL = 64
 
 
 def tile_picked_sidegate_sigmoid_l_kernel(tc, xT, side, w1_words, w1_scales, offs, out):
@@ -40,51 +41,44 @@ def tile_picked_sidegate_sigmoid_l_kernel(tc, xT, side, w1_words, w1_scales, off
         gates = [keep.tile([P, S], F32, name=f"gate{b}") for b in range(N // P)]
         zero = keep.tile([P, 1], F32, name="zero")
 
-        def load_scales(q, queue):
-            queue.dma_start(
-                out=w_scales[32 * q : 32 * q + 4, :].bitcast(I32),
+        for q in range(P // QUADRANT):
+            nc.scalar.dma_start(
+                out=w_scales[QUADRANT * q : QUADRANT * q + 4, :].bitcast(I32),
                 in_=w1_scales[0, 4 * q : 4 * q + 4, :].bitcast(I32),
             )
-
-        def load_words(queue):
-            queue.dma_start(
-                out=w_codes[:].bitcast(I32),
-                in_=w1_words[0].rearrange("p n t -> p (n t)").bitcast(I32),
-            )
-
-        def warm_up():
-            nc.vector.memset(zero[:], 0.0)
-            nc.scalar.activation(gates[0][:, 0:1], zero[:], SIGMOID)
-
-        for q in range(4):
-            load_scales(q, nc.scalar)
         nc.sync.dma_start(out=planes[0][:], in_=x_rows[:, 0, :])
         nc.sync.dma_start(offsets[:], offs)
-        for t in (1, 2, 3):
+        for t in range(1, PACK):
             nc.sync.dma_start(out=planes[t][:], in_=x_rows[:, t, :])
         nc.sync.dma_start(out=sides[0][:], in_=side[0:P, :])
-        load_words(nc.sync)
+        nc.sync.dma_start(
+            out=w_codes[:].bitcast(I32),
+            in_=w1_words[0].rearrange("p n t -> p (n t)").bitcast(I32),
+        )
         nc.sync.dma_start(out=sides[1][:], in_=side[P : 2 * P, :])
-        warm_up()
+
+        nc.vector.memset(zero[:], 0.0)
+        nc.scalar.activation(gates[0][:, 0:1], zero[:], SIGMOID)
 
         def entries(lo, hi):
             return offsets[:, lo // LANES : hi // LANES]
 
         x_codes = keep.tile([P, S], U32, name="x_codes", align_bytes=64)
         x_scales = keep.tile([P, S], U8, name="x_scales", align_bytes=64)
-        low = [keep.tile([P, 2, S - DIRECT], BF16, name=f"low{u}") for u in range(2)]
+        low = [keep.tile([P, 2, S - DIRECT], BF16, name=f"low{pair}") for pair in range(PACK // 2)]
         woven = keep.tile([P, S, PACK], BF16, name="woven", align_bytes=64)
 
         for t in range(PACK):
-            u = t // 2
+            pair = t // 2
             nc.vector.tensor_copy(woven[:, 0:DIRECT, t], planes[t][:].indirect(entries(0, DIRECT)))
             cuts = (DIRECT, MIDDLE, S) if t == PACK - 1 else (DIRECT, S)
             for lo, hi in zip(cuts, cuts[1:]):
                 part = slice(lo - DIRECT, hi - DIRECT)
-                nc.scalar.activation(low[u][:, t % 2, part], planes[t][:].indirect(entries(lo, hi)), COPY)
+                nc.scalar.activation(low[pair][:, t % 2, part], planes[t][:].indirect(entries(lo, hi)), COPY)
                 if t % 2 == 1:
                     nc.vector.tensor_copy(
-                        woven[:, lo:hi, 2 * u : 2 * u + 2], low[u][:, :, part].rearrange("p t s -> p s t")
+                        woven[:, lo:hi, 2 * pair : 2 * pair + 2],
+                        low[pair][:, :, part].rearrange("p t s -> p s t"),
                     )
         for lo in (0, HALF):
             nc.vector.quantize_mx(
@@ -95,33 +89,31 @@ def tile_picked_sidegate_sigmoid_l_kernel(tc, xT, side, w1_words, w1_scales, off
 
         results = [keep.tile([P, S], F32, name=f"result{b}") for b in range(N // P)]
 
-        def gate(b, lo, hi):
-            nc.scalar.activation(gates[b][:, lo:hi], sides[b][:].indirect(entries(lo, hi)), SIGMOID)
-
-        def product(b, lo, hi):
-            acc = psum.tile([P, hi - lo], F32, name=f"acc{b}_{lo}")
-            nc.tensor.matmul_mx(
-                out=acc[:],
-                lhsT=w_codes[:, b * P : (b + 1) * P].bitcast(FP8X4),
-                lhsT_scale=w_scales[:, b * P : (b + 1) * P],
-                rhs=x_codes[:, lo:hi].bitcast(FP8X4),
-                rhs_scale=x_scales[:, lo:hi],
-                start=True,
-                stop=True,
-            )
-            return acc
-
-        def store(b, lo, hi):
-            nc.sync.dma_start(out=out[b * P : (b + 1) * P, lo:hi], in_=results[b][:, lo:hi])
-
-        for lo in (0, HALF):
-            gate(0, lo, lo + HALF)
-        for lo, hi in zip(LAST_CUTS, LAST_CUTS[1:]):
-            gate(1, lo, hi)
+        pieces = [
+            [(0, HALF), (HALF, S)],
+            [(0, HALF), (HALF, S - TAIL), (S - TAIL, S)],
+        ]
         for b in range(N // P):
-            for lo in (0, HALF):
-                acc = product(b, lo, lo + HALF)
-                cuts = LAST_CUTS[1:] if b == 1 and lo == HALF else (lo, lo + HALF)
-                for c0, c1 in zip(cuts, cuts[1:]):
-                    nc.vector.tensor_tensor(results[b][:, c0:c1], acc[:, c0 - lo : c1 - lo], gates[b][:, c0:c1], MULT)
-                store(b, lo, lo + HALF)
+            for lo, hi in pieces[b]:
+                nc.scalar.activation(gates[b][:, lo:hi], sides[b][:].indirect(entries(lo, hi)), SIGMOID)
+
+        for b in range(N // P):
+            rows = slice(b * P, (b + 1) * P)
+            for first in (0, HALF):
+                half = slice(first, first + HALF)
+                acc = psum.tile([P, HALF], F32, name=f"acc{b}_{first}")
+                nc.tensor.matmul_mx(
+                    out=acc[:],
+                    lhsT=w_codes[:, rows].bitcast(FP8X4),
+                    lhsT_scale=w_scales[:, rows],
+                    rhs=x_codes[:, half].bitcast(FP8X4),
+                    rhs_scale=x_scales[:, half],
+                    start=True,
+                    stop=True,
+                )
+                for lo, hi in pieces[b]:
+                    if first <= lo < first + HALF:
+                        nc.vector.tensor_tensor(
+                            results[b][:, lo:hi], acc[:, lo - first : hi - first], gates[b][:, lo:hi], MULT
+                        )
+                nc.sync.dma_start(out=out[rows, half], in_=results[b][:, half])

@@ -21,9 +21,11 @@ PACK = 4
 QUADRANT = 32
 LANES = 16
 HALF = S // 2
+QUARTER = S // 4
 DIRECT = 224
 MIDDLE = 384
 TAIL = 64
+SHARE = 128
 
 
 def tile_picked_sidegate_sigmoid_l_kernel(tc, xT, side, w1_words, w1_scales, offs, out):
@@ -89,31 +91,39 @@ def tile_picked_sidegate_sigmoid_l_kernel(tc, xT, side, w1_words, w1_scales, off
 
         results = [keep.tile([P, S], F32, name=f"result{b}") for b in range(N // P)]
 
-        pieces = [
-            [(0, HALF), (HALF, S)],
-            [(0, HALF), (HALF, S - TAIL), (S - TAIL, S)],
-        ]
+        shared = keep.tile([P, SHARE], F32, name="shared")
+        nc.vector.tensor_copy(shared[:], sides[1][:].indirect(entries(S - SHARE, S)))
+        gate_cuts = [(0, HALF, S), (0, HALF, S - QUARTER, S - TAIL, S)]
         for b in range(N // P):
-            for lo, hi in pieces[b]:
-                nc.scalar.activation(gates[b][:, lo:hi], sides[b][:].indirect(entries(lo, hi)), SIGMOID)
+            for lo, hi in zip(gate_cuts[b], gate_cuts[b][1:]):
+                if b == 1 and lo >= S - SHARE:
+                    picked = shared[:, lo - (S - SHARE) : hi - (S - SHARE)]
+                else:
+                    picked = sides[b][:].indirect(entries(lo, hi))
+                nc.scalar.activation(gates[b][:, lo:hi], picked, SIGMOID)
 
+        product_cuts = [(0, QUARTER, HALF, S - QUARTER, S), (0, HALF, S)]
+        store_cuts = [(HALF, S), (HALF, S)]
         for b in range(N // P):
             rows = slice(b * P, (b + 1) * P)
-            for first in (0, HALF):
-                half = slice(first, first + HALF)
-                acc = psum.tile([P, HALF], F32, name=f"acc{b}_{first}")
+            cuts = sorted(set(gate_cuts[b]) | set(product_cuts[b]) | set(store_cuts[b]))
+            stored = 0
+            for first, last in zip(product_cuts[b], product_cuts[b][1:]):
+                acc = psum.tile([P, last - first], F32, name=f"acc{b}_{first}")
                 nc.tensor.matmul_mx(
                     out=acc[:],
                     lhsT=w_codes[:, rows].bitcast(FP8X4),
                     lhsT_scale=w_scales[:, rows],
-                    rhs=x_codes[:, half].bitcast(FP8X4),
-                    rhs_scale=x_scales[:, half],
+                    rhs=x_codes[:, first:last].bitcast(FP8X4),
+                    rhs_scale=x_scales[:, first:last],
                     start=True,
                     stop=True,
                 )
-                for lo, hi in pieces[b]:
-                    if first <= lo < first + HALF:
+                for lo, hi in zip(cuts, cuts[1:]):
+                    if first <= lo < last:
                         nc.vector.tensor_tensor(
                             results[b][:, lo:hi], acc[:, lo - first : hi - first], gates[b][:, lo:hi], MULT
                         )
-                nc.sync.dma_start(out=out[rows, half], in_=results[b][:, half])
+                        if hi in store_cuts[b]:
+                            nc.sync.dma_start(out=out[rows, stored:hi], in_=results[b][:, stored:hi])
+                            stored = hi

@@ -43,16 +43,16 @@ def tile_picked_sidegate_sigmoid_l_kernel(tc, xT, side, w1_words, w1_scales, off
         gates = [keep.tile([P, S], F32, name=f"gate{b}") for b in range(N // P)]
         zero = keep.tile([P, 1], F32, name="zero")
 
-        for q in range(P // QUADRANT):
-            nc.scalar.dma_start(
-                out=w_scales[QUADRANT * q : QUADRANT * q + 4, :].bitcast(I32),
-                in_=w1_scales[0, 4 * q : 4 * q + 4, :].bitcast(I32),
-            )
         nc.sync.dma_start(out=planes[0][:], in_=x_rows[:, 0, :])
         nc.sync.dma_start(offsets[:], offs)
         for t in range(1, PACK):
             nc.sync.dma_start(out=planes[t][:], in_=x_rows[:, t, :])
         nc.sync.dma_start(out=sides[0][:], in_=side[0:P, :])
+        for q in range(P // QUADRANT):
+            nc.sync.dma_start(
+                out=w_scales[QUADRANT * q : QUADRANT * q + 4, :].bitcast(I32),
+                in_=w1_scales[0, 4 * q : 4 * q + 4, :].bitcast(I32),
+            )
         nc.sync.dma_start(
             out=w_codes[:].bitcast(I32),
             in_=w1_words[0].rearrange("p n t -> p (n t)").bitcast(I32),
@@ -93,7 +93,7 @@ def tile_picked_sidegate_sigmoid_l_kernel(tc, xT, side, w1_words, w1_scales, off
 
         shared = keep.tile([P, SHARE], F32, name="shared")
         nc.vector.tensor_copy(shared[:], sides[1][:].indirect(entries(S - SHARE, S)))
-        gate_cuts = [(0, HALF, S), (0, HALF, S - QUARTER, S - TAIL, S)]
+        gate_cuts = [(0, S - QUARTER, S), (0, HALF, S - QUARTER, S - TAIL, S)]
         for b in range(N // P):
             for lo, hi in zip(gate_cuts[b], gate_cuts[b][1:]):
                 if b == 1 and lo >= S - SHARE:

@@ -21,11 +21,9 @@ PACK = 4
 QUADRANT = 32
 LANES = 16
 HALF = S // 2
-QUARTER = S // 4
 DIRECT = 224
 MIDDLE = 384
-TAIL = 64
-SHARE = 128
+GATE_PIECES = [((0, 384, False), (384, 512, False)), ((0, 192, False), (192, 256, False), (256, 320, False), (320, 416, True), (416, 512, True))]
 
 
 def tile_picked_sidegate_sigmoid_l_kernel(tc, xT, side, w1_words, w1_scales, offs, out):
@@ -43,20 +41,23 @@ def tile_picked_sidegate_sigmoid_l_kernel(tc, xT, side, w1_words, w1_scales, off
         gates = [keep.tile([P, S], F32, name=f"gate{b}") for b in range(N // P)]
         zero = keep.tile([P, 1], F32, name="zero")
 
+        def load_weights():
+            for q in range(P // QUADRANT):
+                nc.sync.dma_start(
+                    out=w_scales[QUADRANT * q : QUADRANT * q + 4, :].bitcast(I32),
+                    in_=w1_scales[0, 4 * q : 4 * q + 4, :].bitcast(I32),
+                )
+            nc.sync.dma_start(
+                out=w_codes[:].bitcast(I32),
+                in_=w1_words[0].rearrange("p n t -> p (n t)").bitcast(I32),
+            )
+
         nc.sync.dma_start(out=planes[0][:], in_=x_rows[:, 0, :])
         nc.sync.dma_start(offsets[:], offs)
         for t in range(1, PACK):
             nc.sync.dma_start(out=planes[t][:], in_=x_rows[:, t, :])
         nc.sync.dma_start(out=sides[0][:], in_=side[0:P, :])
-        for q in range(P // QUADRANT):
-            nc.sync.dma_start(
-                out=w_scales[QUADRANT * q : QUADRANT * q + 4, :].bitcast(I32),
-                in_=w1_scales[0, 4 * q : 4 * q + 4, :].bitcast(I32),
-            )
-        nc.sync.dma_start(
-            out=w_codes[:].bitcast(I32),
-            in_=w1_words[0].rearrange("p n t -> p (n t)").bitcast(I32),
-        )
+        load_weights()
         nc.sync.dma_start(out=sides[1][:], in_=side[P : 2 * P, :])
 
         nc.vector.memset(zero[:], 0.0)
@@ -90,40 +91,36 @@ def tile_picked_sidegate_sigmoid_l_kernel(tc, xT, side, w1_words, w1_scales, off
             )
 
         results = [keep.tile([P, S], F32, name=f"result{b}") for b in range(N // P)]
-
-        shared = keep.tile([P, SHARE], F32, name="shared")
-        nc.vector.tensor_copy(shared[:], sides[1][:].indirect(entries(S - SHARE, S)))
-        gate_cuts = [(0, S - QUARTER, S), (0, HALF, S - QUARTER, S - TAIL, S)]
-        for b in range(N // P):
-            for lo, hi in zip(gate_cuts[b], gate_cuts[b][1:]):
-                if b == 1 and lo >= S - SHARE:
-                    picked = shared[:, lo - (S - SHARE) : hi - (S - SHARE)]
-                else:
-                    picked = sides[b][:].indirect(entries(lo, hi))
-                nc.scalar.activation(gates[b][:, lo:hi], picked, SIGMOID)
-
-        product_cuts = [(0, QUARTER, HALF, S - QUARTER, S), (0, HALF, S)]
-        store_cuts = [(HALF, S), (HALF, S)]
+        picked = [keep.tile([P, S], F32, name=f"picked{b}") for b in range(N // P)]
+        widths = (128, 256)
+        banks = {}
         for b in range(N // P):
             rows = slice(b * P, (b + 1) * P)
-            cuts = sorted(set(gate_cuts[b]) | set(product_cuts[b]) | set(store_cuts[b]))
-            stored = 0
-            for first, last in zip(product_cuts[b], product_cuts[b][1:]):
-                acc = psum.tile([P, last - first], F32, name=f"acc{b}_{first}")
+            for first in range(0, S, widths[b]):
+                acc = psum.tile([P, widths[b]], F32, name=f"acc{b}_{first}")
+                banks[b, first] = acc
                 nc.tensor.matmul_mx(
                     out=acc[:],
                     lhsT=w_codes[:, rows].bitcast(FP8X4),
                     lhsT_scale=w_scales[:, rows],
-                    rhs=x_codes[:, first:last].bitcast(FP8X4),
-                    rhs_scale=x_scales[:, first:last],
+                    rhs=x_codes[:, first : first + widths[b]].bitcast(FP8X4),
+                    rhs_scale=x_scales[:, first : first + widths[b]],
                     start=True,
                     stop=True,
                 )
-                for lo, hi in zip(cuts, cuts[1:]):
-                    if first <= lo < last:
-                        nc.vector.tensor_tensor(
-                            results[b][:, lo:hi], acc[:, lo - first : hi - first], gates[b][:, lo:hi], MULT
-                        )
-                        if hi in store_cuts[b]:
-                            nc.sync.dma_start(out=out[rows, stored:hi], in_=results[b][:, stored:hi])
-                            stored = hi
+
+        for b in range(N // P):
+            rows = slice(b * P, (b + 1) * P)
+            if b == 1:
+                nc.vector.tensor_copy(picked[b][:, 320:S], sides[b][:].indirect(entries(320, S)))
+            for lo, hi, by_vector in GATE_PIECES[b]:
+                source = picked[b][:, lo:hi] if by_vector else sides[b][:].indirect(entries(lo, hi))
+                nc.scalar.activation(gates[b][:, lo:hi], source, SIGMOID)
+                cuts = sorted({lo, hi} | {c for c in range(0, S, widths[b]) if lo < c < hi})
+                for first, last in zip(cuts, cuts[1:]):
+                    start = first - first % widths[b]
+                    nc.vector.tensor_tensor(
+                        results[b][:, first:last], banks[b, start][:, first - start : last - start], gates[b][:, first:last], MULT
+                    )
+                    if last % HALF == 0:
+                        nc.sync.dma_start(out=out[rows, last - HALF : last], in_=results[b][:, last - HALF : last])

@@ -21,9 +21,10 @@ PACK = 4
 QUADRANT = 32
 LANES = 16
 HALF = S // 2
-DIRECT = 224
-MIDDLE = 384
-GATE_PIECES = [((0, 384, False), (384, 512, False)), ((0, 192, False), (192, 256, False), (256, 320, False), (320, 416, True), (416, 512, True))]
+DIRECT = (224, 128)
+LAST_CUTS = (128, 256, 384, 512)
+QUANTISE_CUTS = (0, 128, 256, 384, 512)
+GATE_PIECES = [((0, 384, False), (384, 512, False)), ((0, 256, False), (256, 384, False), (384, 448, True), (448, 512, True))]
 
 
 def tile_picked_sidegate_sigmoid_l_kernel(tc, xT, side, w1_words, w1_scales, offs, out):
@@ -68,26 +69,26 @@ def tile_picked_sidegate_sigmoid_l_kernel(tc, xT, side, w1_words, w1_scales, off
 
         x_codes = keep.tile([P, S], U32, name="x_codes", align_bytes=64)
         x_scales = keep.tile([P, S], U8, name="x_scales", align_bytes=64)
-        low = [keep.tile([P, 2, S - DIRECT], BF16, name=f"low{pair}") for pair in range(PACK // 2)]
+        low = [keep.tile([P, 2, S], BF16, name=f"low{pair}") for pair in range(PACK // 2)]
         woven = keep.tile([P, S, PACK], BF16, name="woven", align_bytes=64)
 
         for t in range(PACK):
             pair = t // 2
-            nc.vector.tensor_copy(woven[:, 0:DIRECT, t], planes[t][:].indirect(entries(0, DIRECT)))
-            cuts = (DIRECT, MIDDLE, S) if t == PACK - 1 else (DIRECT, S)
+            direct = DIRECT[pair]
+            nc.vector.tensor_copy(woven[:, 0:direct, t], planes[t][:].indirect(entries(0, direct)))
+            cuts = LAST_CUTS if t == PACK - 1 else (direct, S)
             for lo, hi in zip(cuts, cuts[1:]):
-                part = slice(lo - DIRECT, hi - DIRECT)
-                nc.scalar.activation(low[pair][:, t % 2, part], planes[t][:].indirect(entries(lo, hi)), COPY)
+                nc.scalar.activation(low[pair][:, t % 2, lo:hi], planes[t][:].indirect(entries(lo, hi)), COPY)
                 if t % 2 == 1:
                     nc.vector.tensor_copy(
                         woven[:, lo:hi, 2 * pair : 2 * pair + 2],
-                        low[pair][:, :, part].rearrange("p t s -> p s t"),
+                        low[pair][:, :, lo:hi].rearrange("p t s -> p s t"),
                     )
-        for lo in (0, HALF):
+        for lo, hi in zip(QUANTISE_CUTS, QUANTISE_CUTS[1:]):
             nc.vector.quantize_mx(
-                out=x_codes[:, lo : lo + HALF].bitcast(FP8X4),
-                scales=x_scales[:, lo : lo + HALF],
-                in_=woven[:, lo : lo + HALF, :].rearrange("p s t -> p (s t)"),
+                out=x_codes[:, lo:hi].bitcast(FP8X4),
+                scales=x_scales[:, lo:hi],
+                in_=woven[:, lo:hi, :].rearrange("p s t -> p (s t)"),
             )
 
         results = [keep.tile([P, S], F32, name=f"result{b}") for b in range(N // P)]
@@ -112,7 +113,7 @@ def tile_picked_sidegate_sigmoid_l_kernel(tc, xT, side, w1_words, w1_scales, off
         for b in range(N // P):
             rows = slice(b * P, (b + 1) * P)
             if b == 1:
-                nc.vector.tensor_copy(picked[b][:, 320:S], sides[b][:].indirect(entries(320, S)))
+                nc.vector.tensor_copy(picked[b][:, 384:S], sides[b][:].indirect(entries(384, S)))
             for lo, hi, by_vector in GATE_PIECES[b]:
                 source = picked[b][:, lo:hi] if by_vector else sides[b][:].indirect(entries(lo, hi))
                 nc.scalar.activation(gates[b][:, lo:hi], source, SIGMOID)

from contextlib import ExitStack

import concourse.mybir as mybir

K, T, S, N = 512, 1024, 512, 256
FLOPS = 2 * K * S * N

F32 = mybir.dt.float32
BF16 = mybir.dt.bfloat16
I32 = mybir.dt.int32
U32 = mybir.dt.uint32
U16 = mybir.dt.uint16
U8 = mybir.dt.uint8
FP8X4 = mybir.dt.float8_e4m3fn_x4
SIGMOID = mybir.ActivationFunctionType.Sigmoid
COPY = mybir.ActivationFunctionType.Copy
MULT = mybir.AluOpType.mult

P = 128
PACK = 4
QUADRANT = 32
LANES = 16
HALF = S // 2
DIRECT = (224, 128)
LAST_CUTS = (128, 256, 384, 512)
QUANTISE_CUTS = (0, 128, 256, 384, 512)
GATE_PIECES = [((0, 384, False), (384, 512, False)), ((0, 256, False), (256, 384, False), (384, 448, True), (448, 512, True))]


def tile_picked_sidegate_sigmoid_l_kernel(tc, xT, side, w1_words, w1_scales, offs, out):
    nc = tc.nc
    with ExitStack() as ctx:
        keep = ctx.enter_context(tc.tile_pool(name="keep", bufs=1))
        psum = ctx.enter_context(tc.psum_pool(name="psum", bufs=1))

        offsets = keep.tile([P, S // LANES], U16, name="offsets")
        planes = [keep.tile([P, T], F32, name=f"plane{t}") for t in range(PACK)]
        sides = [keep.tile([P, T], F32, name=f"side{b}") for b in range(N // P)]
        w_codes = keep.tile([P, N], U32, name="w_codes", align_bytes=64)
        w_scales = keep.tile([P, N], U8, name="w_scales", align_bytes=64)
        x_rows = xT.rearrange("(p t) c -> p t c", t=PACK)
        gates = [keep.tile([P, S], F32, name=f"gate{b}") for b in range(N // P)]
        zero = keep.tile([P, 1], F32, name="zero")

        def load_weights():
            for q in range(P // QUADRANT):
                nc.sync.dma_start(
                    out=w_scales[QUADRANT * q : QUADRANT * q + 4, :].bitcast(I32),
                    in_=w1_scales[0, 4 * q : 4 * q + 4, :].bitcast(I32),
                )
            nc.sync.dma_start(
                out=w_codes[:].bitcast(I32),
                in_=w1_words[0].rearrange("p n t -> p (n t)").bitcast(I32),
            )

        nc.sync.dma_start(out=planes[0][:], in_=x_rows[:, 0, :])
        nc.sync.dma_start(offsets[:], offs)
        for t in range(1, PACK):
            nc.sync.dma_start(out=planes[t][:], in_=x_rows[:, t, :])
        nc.sync.dma_start(out=sides[0][:], in_=side[0:P, :])
        load_weights()
        nc.sync.dma_start(out=sides[1][:], in_=side[P : 2 * P, :])

        nc.vector.memset(zero[:], 0.0)
        nc.scalar.activation(gates[0][:, 0:1], zero[:], SIGMOID)

        def entries(lo, hi):
            return offsets[:, lo // LANES : hi // LANES]

        x_codes = keep.tile([P, S], U32, name="x_codes", align_bytes=64)
        x_scales = keep.tile([P, S], U8, name="x_scales", align_bytes=64)
        low = [keep.tile([P, 2, S], BF16, name=f"low{pair}") for pair in range(PACK // 2)]
        woven = keep.tile([P, S, PACK], BF16, name="woven", align_bytes=64)

        for t in range(PACK):
            pair = t // 2
            direct = DIRECT[pair]
            nc.vector.tensor_copy(woven[:, 0:direct, t], planes[t][:].indirect(entries(0, direct)))
            cuts = LAST_CUTS if t == PACK - 1 else (direct, S)
            for lo, hi in zip(cuts, cuts[1:]):
                nc.scalar.activation(low[pair][:, t % 2, lo:hi], planes[t][:].indirect(entries(lo, hi)), COPY)
                if t % 2 == 1:
                    nc.vector.tensor_copy(
                        woven[:, lo:hi, 2 * pair : 2 * pair + 2],
                        low[pair][:, :, lo:hi].rearrange("p t s -> p s t"),
                    )
        for lo, hi in zip(QUANTISE_CUTS, QUANTISE_CUTS[1:]):
            nc.vector.quantize_mx(
                out=x_codes[:, lo:hi].bitcast(FP8X4),
                scales=x_scales[:, lo:hi],
                in_=woven[:, lo:hi, :].rearrange("p s t -> p (s t)"),
            )

        results = [keep.tile([P, S], F32, name=f"result{b}") for b in range(N // P)]
        picked = [keep.tile([P, S], F32, name=f"picked{b}") for b in range(N // P)]
        widths = (128, 256)
        banks = {}
        for b in range(N // P):
            rows = slice(b * P, (b + 1) * P)
            for first in range(0, S, widths[b]):
                acc = psum.tile([P, widths[b]], F32, name=f"acc{b}_{first}")
                banks[b, first] = acc
                nc.tensor.matmul_mx(
                    out=acc[:],
                    lhsT=w_codes[:, rows].bitcast(FP8X4),
                    lhsT_scale=w_scales[:, rows],
                    rhs=x_codes[:, first : first + widths[b]].bitcast(FP8X4),
                    rhs_scale=x_scales[:, first : first + widths[b]],
                    start=True,
                    stop=True,
                )

        for b in range(N // P):
            rows = slice(b * P, (b + 1) * P)
            if b == 1:
                nc.vector.tensor_copy(picked[b][:, 384:S], sides[b][:].indirect(entries(384, S)))
            for lo, hi, by_vector in GATE_PIECES[b]:
                source = picked[b][:, lo:hi] if by_vector else sides[b][:].indirect(entries(lo, hi))
                nc.scalar.activation(gates[b][:, lo:hi], source, SIGMOID)
                cuts = sorted({lo, hi} | {c for c in range(0, S, widths[b]) if lo < c < hi})
                for first, last in zip(cuts, cuts[1:]):
                    start = first - first % widths[b]
                    nc.vector.tensor_tensor(
                        results[b][:, first:last], banks[b, start][:, first - start : last - start], gates[b][:, first:last], MULT
                    )
                    if last % HALF == 0:
                        nc.sync.dma_start(out=out[rows, last - HALF : last], in_=results[b][:, last - HALF : last])
